import numpy as np
import ml_dtypes


def mxq(x, axis, fmt="e4m3"):
    dtype, down = {"e4m3": (ml_dtypes.float8_e4m3fn, 7), "e5m2": (ml_dtypes.float8_e5m2, 14)}[fmt]
    v = np.moveaxis(np.asarray(x, np.float32).astype(ml_dtypes.bfloat16).astype(np.float64), axis, -1)
    blocks = v.reshape(v.shape[:-1] + (-1, 32))
    amax = np.abs(blocks).max(-1, keepdims=True)
    byte = np.maximum(np.where(amax > 0, np.frexp(amax)[1] - 1 + 127, 0) - down, 1)
    scale = np.exp2(byte - 127.0)
    codes = (blocks / scale).astype(np.float32).astype(dtype).astype(np.float64)
    return np.moveaxis((codes * scale).reshape(v.shape), -1, axis)


WIDE = False


def mx_kscale(k):
    if not WIDE:
        return np.ones(k)
    levels = np.array([10, -10, 5, -5, 0])
    if k % 512:
        return np.exp2(np.random.permutation(np.resize(levels, k // 32))).repeat(32)
    a = np.empty((k // 512, 16))
    for p in range(k // 512):
        a[p, :8] = np.random.permutation(np.resize(levels, 8))
        for g in range(8):
            far = levels[np.abs(levels - a[p, g]) >= 10]
            a[p, g + 8] = far[np.random.randint(len(far))]
    return np.exp2(a.ravel()).repeat(32)


def f64(x):
    return np.asarray(x).astype(np.float64)


def striped(idx):
    return np.tile(idx.reshape(-1, 16).T, (8, 1)).astype(np.uint16)


def unstriped(offs):
    return offs[:16].T.reshape(-1).astype(np.int64)


def striped8(idx):
    return np.concatenate([x.reshape(-1, 16).T for x in idx]).astype(np.uint16)


def runs(offs, k):
    lists = np.stack([offs[16 * r : 16 * r + 16].T.reshape(-1) for r in range(8)]).astype(np.int64)
    return lists[np.arange(k) % 512 // 64]


def pack_weight(w):
    k, n = w.shape
    w = f64(np.asarray(w, np.float32).astype(ml_dtypes.bfloat16)).reshape(k // 32, 32, n)
    amax = np.abs(w).max(1)
    byte = np.clip(np.where(amax > 0, np.frexp(amax)[1] - 1 + 127 - 7, 1), 1, 254)
    scaled = (w * np.exp2(127.0 - byte)[:, None, :]).reshape(k, n).astype(np.float32)
    words = np.ascontiguousarray(scaled.reshape(k // 512, 128, 4, n).transpose(0, 1, 3, 2)).astype(ml_dtypes.float8_e4m3fn).view(np.uint8)
    return words, np.ascontiguousarray(byte.astype(np.uint8).reshape(k // 512, 16, n))


def unpack_weight(words, scales):
    g, p, n, _ = words.shape
    vals = np.ascontiguousarray(words).view(ml_dtypes.float8_e4m3fn).astype(np.float64) * np.repeat(np.exp2(scales.astype(np.float64) - 127.0), 8, axis=1)[..., None]
    return vals.transpose(0, 1, 3, 2).reshape(g * 512, n)


K, T, S, N, H = 512, 2048, 512, 512, 512


def setup_inputs():
    n = np.random.standard_normal
    s = mx_kscale(K)[:, None]
    u = mx_kscale(H)
    packed_xT = pack_weight(n((K, T)) * s)
    return {
        "x_words": packed_xT[0],
        "x_scales": packed_xT[1],
        "w1": (n((K, H)) / np.sqrt(K) / s).astype(np.float32),
        "gn": (np.random.uniform(0.5, 1.5, (H, 1)) * u[:, None]).astype(np.float32),
        "w2": (n((H, N)) / np.sqrt(H) / u[:, None]).astype(np.float32),
        "offs": striped(np.random.permutation(T)[:S]),
        "p1": striped8(np.stack([np.random.permutation(S) for _ in range(8)])),
        "p2": striped8(np.stack([np.random.permutation(S) for _ in range(8)])),
    }


def reference(x_words, x_scales, w1, gn, w2, offs, p1, p2):
    xq = unpack_weight(x_words, x_scales)[:, unstriped(offs)]
    y = mxq(f64(w1), 0, "e4m3").T @ xq
    a = y[np.arange(H)[:, None], runs(p1, H)]
    b = y[np.arange(H)[:, None], runs(p2, H)]
    mu = 0.3125 * (y + a + b)
    vr = (y - mu) ** 2 + (a - mu) ** 2 + (b - mu) ** 2
    z = f64(gn) * ((y - mu) / np.sqrt(0.25 * vr + 0.1))
    return mxq(f64(w2), 0, "e4m3").T @ mxq(z, 0, "e4m3")

@@ -1,0 +1,224 @@
+from contextlib import ExitStack
+import math
+
+import concourse.mybir as mybir
+from concourse.masks import make_identity
+
+K, T, S, N, H = 512, 2048, 512, 512, 512
+FLOPS = 2 * K * H * S + 2 * H * N * S
+
+F32 = mybir.dt.float32
+BF16 = mybir.dt.bfloat16
+U32 = mybir.dt.uint32
+I32 = mybir.dt.int32
+U16 = mybir.dt.uint16
+U8 = mybir.dt.uint8
+FP8X4 = mybir.dt.float8_e4m3fn_x4
+ALU = mybir.AluOpType
+ACT = mybir.ActivationFunctionType
+
+P = 128
+PACK = 4
+BLOCK = 128
+HALF = 256
+
+C_MU = 0.3125
+K_S = 2 * C_MU - 3 * C_MU * C_MU
+A_R = 0.5 - K_S
+LAM = -K_S / A_R
+B_Y = (1 - K_S) - K_S * K_S / A_R
+SC_D = math.sqrt(0.25 * 0.5)
+SC_R = math.sqrt(0.25 * A_R)
+SC_Y = math.sqrt(0.25 * B_Y)
+
+
+def tile_picked_zscore3_none_p_kernel(tc, x_words, x_scales, w1, gn, w2, offs, p1, p2, out):
+    nc = tc.nc
+    with ExitStack() as ctx:
+        keep = ctx.enter_context(tc.tile_pool(name="keep", bufs=1))
+        psum = ctx.enter_context(tc.psum_pool(name="psum", bufs=1))
+
+        offs_t = keep.tile([P, S // 16], U16, name="offs_t")
+        p1_t = keep.tile([P, S // 16], U16, name="p1_t")
+        p2_t = keep.tile([P, S // 16], U16, name="p2_t")
+        xs_all = keep.tile([P, T], U8, name="xs_all")
+        xw_all = keep.tile([P, T], U32, name="xw_all")
+        w1_raw = keep.tile([P, PACK, H], F32, name="w1_raw")
+        w2_raw = keep.tile([P, PACK, N], F32, name="w2_raw")
+        gn_t = keep.tile([P, PACK], F32, name="gn_t")
+
+        nc.gpsimd.memset(xs_all[:].bitcast(I32), 0)
+        nc.sync.dma_start(offs_t[:], offs)
+        nc.sync.dma_start(w1_raw[:], w1.rearrange("(p j) c -> p j c", j=PACK))
+        for q in range(4):
+            nc.sync.dma_start(xs_all[q:P:32, :].bitcast(I32), x_scales[0, q:16:4, :].bitcast(I32))
+        nc.sync.dma_start(xw_all[:].bitcast(I32), x_words[0].rearrange("p n t -> p (n t)").bitcast(I32))
+        nc.sync.dma_start(p1_t[:], p1)
+        nc.sync.dma_start(p2_t[:], p2)
+        nc.sync.dma_start(gn_t[:], gn.rearrange("(p t) o -> p (t o)", t=PACK))
+        nc.sync.dma_start(w2_raw[:], w2.rearrange("(p j) c -> p j c", j=PACK))
+
+        warm = keep.tile([P, 2], F32, name="warm")
+        nc.vector.memset(warm[:, 0:1], 1.0)
+        nc.scalar.activation(warm[:, 1:2], warm[:, 0:1], ACT.Abs_reciprocal_sqrt)
+
+        ident = keep.tile([P, P], F32, name="ident")
+        make_identity(nc, ident[:])
+
+        xs = keep.tile([P, S], U8, name="xs", align_bytes=64)
+        xw = keep.tile([P, S], U32, name="xw", align_bytes=64)
+        nc.vector.tensor_copy(xs[:], xs_all[:].indirect(offs_t[:]))
+
+        w1_src = w1_raw[:].rearrange("p j (m t) -> p m j t", t=PACK)
+        w1_codes, w1_scales = [], []
+        w1_bf = []
+        for h in range(2):
+            b = keep.tile([P, 2 * P * PACK], BF16, name="w1_bf%d" % h, align_bytes=64)
+            dst = b[:].rearrange("p (t m j) -> p m j t", t=2, j=PACK)
+            if h == 0:
+                nc.vector.tensor_copy(dst, w1_src[:, :, :, 0:2])
+            else:
+                nc.scalar.copy(dst, w1_src[:, :, :, 2:4])
+            w1_bf.append(b)
+        for h in range(2):
+            c = keep.tile([P, 2 * P], U32, name="w1_c%d" % h, align_bytes=64)
+            s = keep.tile([P, 2 * P], U8, name="w1_s%d" % h, align_bytes=64)
+            nc.vector.quantize_mx(out=c[:].bitcast(FP8X4), scales=s[:], in_=w1_bf[h][:])
+            w1_codes.append(c)
+            w1_scales.append(s)
+        g_u = keep.tile([P, PACK], F32, name="g_u")
+        g_y = keep.tile([P, PACK], F32, name="g_y")
+        nc.vector.tensor_scalar(g_u[:], gn_t[:], -C_MU, None, ALU.mult)
+        nc.vector.tensor_scalar(g_y[:], gn_t[:], 1 - C_MU, None, ALU.mult)
+        for h in range(2):
+            nc.vector.tensor_copy(xw[:, h * HALF : (h + 1) * HALF], xw_all[:].indirect(offs_t[:, h * HALF // 16 : (h + 1) * HALF // 16]))
+
+        def project(dst, t, cols):
+            w = slice((t % 2) * P, (t % 2 + 1) * P)
+            nc.tensor.matmul_mx(out=dst, lhsT=w1_codes[t // 2][:, w].bitcast(FP8X4), lhsT_scale=w1_scales[t // 2][:, w],
+                                rhs=xw[:, cols].bitcast(FP8X4), rhs_scale=xs[:, cols], start=True, stop=True)
+
+        y = [keep.tile([P, S], F32, name="y%d" % t) for t in range(PACK)]
+        early = [psum.tile([P, S], F32, name="early", tag="res", bufs=2) for t in range(2)]
+        for t in range(2):
+            project(early[t][:, 0:HALF], t, slice(0, HALF))
+            nc.vector.tensor_copy(y[t][:, 0:HALF], early[t][:, 0:HALF])
+        for t in range(PACK):
+            acc = psum.tile([P, S], F32, name="acc", tag="acc", bufs=4)
+            cols = slice(HALF if t < 2 else 0, S)
+            project(acc[:, cols], t, cols)
+            nc.scalar.copy(y[t][:, cols], acc[:, cols])
+
+        y_sq = keep.tile([P, PACK, S], F32, name="y_sq")
+        y_g = keep.tile([P, PACK, S], F32, name="y_g")
+        a = [keep.tile([P, PACK, HALF], F32, name="a%d" % h) for h in range(2)]
+        d = [keep.tile([P, PACK, HALF], F32, name="d%d" % h) for h in range(2)]
+        u = [keep.tile([P, PACK, HALF], F32, name="u%d" % h) for h in range(2)]
+        r = [keep.tile([P, PACK, HALF], F32, name="r%d" % h) for h in range(2)]
+        n = [keep.tile([P, PACK, HALF], F32, name="n%d" % h) for h in range(2)]
+        d_sq = [keep.tile([P, PACK, HALF], F32, name="d_sq%d" % h) for h in range(2)]
+        r_sq = [keep.tile([P, PACK, BLOCK], F32, name="r_sq%d" % b) for b in range(4)]
+        rs_t = [keep.tile([P, PACK * P], F32, name="rs_t%d" % b) for b in range(4)]
+        v_t = {}
+        rs = {}
+        w2_bf = keep.tile([P, N * PACK], BF16, name="w2_bf", align_bytes=64)
+        w2_codes = keep.tile([P, N], U32, name="w2_codes", align_bytes=64)
+        w2_scales = keep.tile([P, N], U8, name="w2_scales", align_bytes=64)
+
+        def gathers(h):
+            lists = slice(h * HALF // 16, (h + 1) * HALF // 16)
+            for step in range(PACK + 1):
+                if step < PACK:
+                    nc.vector.tensor_copy(a[h][:, step, :], y[step][:].indirect(p1_t[:, lists]))
+                if step > 0:
+                    t = step - 1
+                    nc.vector.tensor_tensor(d[h][:, t, :], y[t][:].indirect(p2_t[:, lists]), a[h][:, t, :], ALU.subtract)
+
+        def forms(h):
+            cols = slice(h * HALF, (h + 1) * HALF)
+            for g in range(2):
+                nc.vector.scalar_tensor_tensor(u[h][:, 2 * g : 2 * g + 2, :], a[h][:, 2 * g : 2 * g + 2, :], 2.0, d[h][:, 2 * g : 2 * g + 2, :], ALU.mult, ALU.add)
+            for t in range(PACK):
+                nc.vector.scalar_tensor_tensor(r[h][:, t, :], y[t][:, cols], LAM, u[h][:, t, :], ALU.mult, ALU.add)
+
+        def numerator(h, ts):
+            cols = slice(h * HALF, (h + 1) * HALF)
+            for t in ts:
+                nc.vector.scalar_tensor_tensor(n[h][:, t, :], u[h][:, t, :], g_u[:, t : t + 1], y_g[:, t, cols], ALU.mult, ALU.add)
+
+        def add_turned(b, src, first, last):
+            for t in range(PACK):
+                nc.tensor.matmul(v_t[b][:, t * P : (t + 1) * P], lhsT=src[:, t, :], rhs=ident[:], is_transpose=True,
+                                 start=(first and t == 0), stop=(last and t == PACK - 1))
+
+        def early_squares(h):
+            nc.scalar.activation(d_sq[h][:], d[h][:], ACT.Square, scale=SC_D)
+            for b in (2 * h, 2 * h + 1):
+                v_t[b] = psum.tile([P, PACK * P], F32, name="v_t", tag="acc", bufs=4)
+                add_turned(b, y_sq[:, :, b * BLOCK : (b + 1) * BLOCK], True, False)
+                add_turned(b, d_sq[h][:, :, (b % 2) * BLOCK : (b % 2 + 1) * BLOCK], False, False)
+
+        def late_squares(h):
+            for b in (2 * h, 2 * h + 1):
+                nc.scalar.activation(r_sq[b][:], r[h][:, :, (b % 2) * BLOCK : (b % 2 + 1) * BLOCK], ACT.Square, scale=SC_R)
+                add_turned(b, r_sq[b][:], False, True)
+
+        def inverse_roots(h):
+            for b in (2 * h, 2 * h + 1):
+                nc.scalar.activation(rs_t[b][:], v_t[b][:], ACT.Abs_reciprocal_sqrt, bias=0.1)
+                rs[b] = psum.tile([P, PACK, BLOCK], F32, name="rs", tag="rs", bufs=2)
+                for t in range(PACK):
+                    nc.tensor.transpose(rs[b][:, t, :], rs_t[b][:, t * P : (t + 1) * P], ident[:])
+
+        z_bf = {}
+
+        def scale_block(b):
+            z_bf[b] = keep.tile([P, BLOCK * PACK], BF16, name="z_bf%d" % b, align_bytes=64)
+            n_b = n[b // 2][:, :, (b % 2) * BLOCK : (b % 2 + 1) * BLOCK]
+            nc.vector.tensor_tensor(z_bf[b][:].rearrange("p (c i t) -> p c t i", i=4, t=PACK),
+                                    rs[b][:].rearrange("p t (c i) -> p c t i", i=4),
+                                    n_b.rearrange("p t (c i) -> p c t i", i=4), ALU.mult)
+
+        def finish_block(b):
+            z_codes = keep.tile([P, BLOCK], U32, name="z_codes%d" % b, align_bytes=64)
+            z_scales = keep.tile([P, BLOCK], U8, name="z_scales%d" % b, align_bytes=64)
+            nc.vector.quantize_mx(out=z_codes[:].bitcast(FP8X4), scales=z_scales[:], in_=z_bf[b][:])
+            res = psum.tile([P, PACK * BLOCK], F32, name="res", tag="res", bufs=2)
+            for m in range(N // P):
+                rows = slice(m * P, (m + 1) * P)
+                nc.tensor.matmul_mx(out=res[:, m * BLOCK : (m + 1) * BLOCK], lhsT=w2_codes[:, rows].bitcast(FP8X4), lhsT_scale=w2_scales[:, rows],
+                                    rhs=z_codes[:].bitcast(FP8X4), rhs_scale=z_scales[:], start=True, stop=True)
+            staged = keep.tile([P, PACK * BLOCK], F32, name="staged%d" % b)
+            if b == 3:
+                nc.vector.tensor_copy(staged[:], res[:])
+            else:
+                nc.scalar.copy(staged[:], res[:])
+            nc.sync.dma_start(out.rearrange("(m p) j -> p m j", p=P)[:, :, b * BLOCK : (b + 1) * BLOCK], staged[:].rearrange("p (m j) -> p m j", m=PACK))
+
+        for t in range(PACK):
+            nc.scalar.activation(y_sq[:, t, :], y[t][:], ACT.Square, scale=SC_Y)
+        for t in range(PACK):
+            nc.scalar.activation(y_g[:, t, :], y[t][:], ACT.Copy, scale=g_y[:, t : t + 1])
+        gathers(0)
+        early_squares(0)
+        forms(0)
+        late_squares(0)
+        nc.scalar.copy(w2_bf[:].rearrange("p (c i j) -> p c j i", i=4, j=PACK), w2_raw[:].rearrange("p j (c i) -> p c j i", i=4))
+        inverse_roots(0)
+        gathers(1)
+        early_squares(1)
+        numerator(0, range(PACK))
+        nc.vector.quantize_mx(out=w2_codes[:].bitcast(FP8X4), scales=w2_scales[:], in_=w2_bf[:])
+        forms(1)
+        late_squares(1)
+        inverse_roots(1)
+        scale_block(0)
+        numerator(1, (0, 1))
+        finish_block(0)
+        scale_block(1)
+        numerator(1, (2, 3))
+        finish_block(1)
+        scale_block(2)
+        scale_block(3)
+        finish_block(2)
+        finish_block(3)

@@ -88,8 +88,8 @@ def tile_picked_zscore3_none_p_kernel(tc, x_words, x_scales, w1, gn, w2, offs, p
             w1_scales.append(s)
         g_u = keep.tile([P, PACK], F32, name="g_u")
         g_y = keep.tile([P, PACK], F32, name="g_y")
-        nc.vector.tensor_scalar(g_u[:], gn_t[:], -C_MU, None, ALU.mult)
-        nc.vector.tensor_scalar(g_y[:], gn_t[:], 1 - C_MU, None, ALU.mult)
+        nc.scalar.activation(g_u[:], gn_t[:], ACT.Copy, scale=-C_MU)
+        nc.scalar.activation(g_y[:], gn_t[:], ACT.Copy, scale=1 - C_MU)
         for h in range(2):
             nc.vector.tensor_copy(xw[:, h * HALF : (h + 1) * HALF], xw_all[:].indirect(offs_t[:, h * HALF // 16 : (h + 1) * HALF // 16]))
 
@@ -98,26 +98,29 @@ def tile_picked_zscore3_none_p_kernel(tc, x_words, x_scales, w1, gn, w2, offs, p
             nc.tensor.matmul_mx(out=dst, lhsT=w1_codes[t // 2][:, w].bitcast(FP8X4), lhsT_scale=w1_scales[t // 2][:, w],
                                 rhs=xw[:, cols].bitcast(FP8X4), rhs_scale=xs[:, cols], start=True, stop=True)
 
-        y = [keep.tile([P, S], F32, name="y%d" % t) for t in range(PACK)]
-        early = [psum.tile([P, S], F32, name="early", tag="res", bufs=2) for t in range(2)]
+        windows = [keep.tile([P, 2 * S], F32, name="window%d" % t) for t in range(PACK)]
+        y = [w[:, 0:S] for w in windows]
+        for w in windows:
+            nc.gpsimd.memset(w[:, S:], 0.0)
         for t in range(2):
-            project(early[t][:, 0:HALF], t, slice(0, HALF))
-            nc.vector.tensor_copy(y[t][:, 0:HALF], early[t][:, 0:HALF])
+            early = psum.tile([P, HALF], F32, name="early", tag="rs%d" % t)
+            project(early[:], t, slice(0, HALF))
+            nc.vector.tensor_copy(y[t][:, 0:HALF], early[:])
         for t in range(PACK):
-            acc = psum.tile([P, S], F32, name="acc", tag="acc", bufs=4)
+            acc = psum.tile([P, S], F32, name="acc", tag="sum%d" % t)
             cols = slice(HALF if t < 2 else 0, S)
             project(acc[:, cols], t, cols)
             nc.scalar.copy(y[t][:, cols], acc[:, cols])
 
         y_sq = keep.tile([P, PACK, S], F32, name="y_sq")
         y_g = keep.tile([P, PACK, S], F32, name="y_g")
-        a = [keep.tile([P, PACK, HALF], F32, name="a%d" % h) for h in range(2)]
-        d = [keep.tile([P, PACK, HALF], F32, name="d%d" % h) for h in range(2)]
-        u = [keep.tile([P, PACK, HALF], F32, name="u%d" % h) for h in range(2)]
-        r = [keep.tile([P, PACK, HALF], F32, name="r%d" % h) for h in range(2)]
-        n = [keep.tile([P, PACK, HALF], F32, name="n%d" % h) for h in range(2)]
-        d_sq = [keep.tile([P, PACK, HALF], F32, name="d_sq%d" % h) for h in range(2)]
-        r_sq = [keep.tile([P, PACK, BLOCK], F32, name="r_sq%d" % b) for b in range(4)]
+        a = keep.tile([P, PACK, S], F32, name="a")
+        d = keep.tile([P, PACK, S], F32, name="d")
+        u = keep.tile([P, PACK, S], F32, name="u")
+        r = keep.tile([P, PACK, S], F32, name="r")
+        n = keep.tile([P, PACK, S], F32, name="n")
+        d_sq = keep.tile([P, PACK, S], F32, name="d_sq")
+        r_sq = keep.tile([P, PACK, S], F32, name="r_sq")
         rs_t = [keep.tile([P, PACK * P], F32, name="rs_t%d" % b) for b in range(4)]
         v_t = {}
         rs = {}
@@ -125,100 +128,107 @@ def tile_picked_zscore3_none_p_kernel(tc, x_words, x_scales, w1, gn, w2, offs, p
         w2_codes = keep.tile([P, N], U32, name="w2_codes", align_bytes=64)
         w2_scales = keep.tile([P, N], U8, name="w2_scales", align_bytes=64)
 
-        def gathers(h):
-            lists = slice(h * HALF // 16, (h + 1) * HALF // 16)
-            for step in range(PACK + 1):
-                if step < PACK:
-                    nc.vector.tensor_copy(a[h][:, step, :], y[step][:].indirect(p1_t[:, lists]))
-                if step > 0:
-                    t = step - 1
-                    nc.vector.tensor_tensor(d[h][:, t, :], y[t][:].indirect(p2_t[:, lists]), a[h][:, t, :], ALU.subtract)
+        def fetch_a(t, cols):
+            nc.vector.tensor_copy(a[:, t, cols], windows[t][:].indirect(p1_t[:, cols.start // 16 : cols.stop // 16]))
 
-        def forms(h):
-            cols = slice(h * HALF, (h + 1) * HALF)
-            for g in range(2):
-                nc.vector.scalar_tensor_tensor(u[h][:, 2 * g : 2 * g + 2, :], a[h][:, 2 * g : 2 * g + 2, :], 2.0, d[h][:, 2 * g : 2 * g + 2, :], ALU.mult, ALU.add)
+        def fetch_sum(t, cols):
+            nc.vector.tensor_tensor(u[:, t, cols], windows[t][:].indirect(p2_t[:, cols.start // 16 : cols.stop // 16]), a[:, t, cols], ALU.add)
+
+        def forms(t, cols):
+            nc.vector.scalar_tensor_tensor(d[:, t, cols], a[:, t, cols], -2.0, u[:, t, cols], ALU.mult, ALU.add)
+            nc.vector.scalar_tensor_tensor(r[:, t, cols], y[t][:, cols], LAM, u[:, t, cols], ALU.mult, ALU.add)
+
+        def squares(t, cols):
+            for form, sq, scale in ((d, d_sq, SC_D), (r, r_sq, SC_R)):
+                nc.scalar.activation(sq[:, t, cols], form[:, t, cols], ACT.Square, scale=scale)
+                for b in range(cols.start // BLOCK, cols.stop // BLOCK):
+                    nc.tensor.matmul(v_t[b][:, t * P : (t + 1) * P], lhsT=sq[:, t, b * BLOCK : (b + 1) * BLOCK], rhs=ident[:],
+                                     is_transpose=True, start=False, stop=form is r and t == PACK - 1)
+
+        def gain(t):
+            nc.scalar.activation(y_g[:, t, :], y[t], ACT.Copy, scale=g_y[:, t : t + 1])
+
+        def numerator(t, cols, place):
+            nc.vector.scalar_tensor_tensor(n[:, t, place], u[:, t, cols], g_u[:, t : t + 1], y_g[:, t, cols], ALU.mult, ALU.add)
+
+        def open_sum(b):
+            v_t[b] = psum.tile([P, PACK * P], F32, name="v_t", tag="sum%d" % b)
             for t in range(PACK):
-                nc.vector.scalar_tensor_tensor(r[h][:, t, :], y[t][:, cols], LAM, u[h][:, t, :], ALU.mult, ALU.add)
+                nc.tensor.matmul(v_t[b][:, t * P : (t + 1) * P], lhsT=y_sq[:, t, b * BLOCK : (b + 1) * BLOCK], rhs=ident[:],
+                                 is_transpose=True, start=t == 0, stop=False)
 
-        def numerator(h, ts):
-            cols = slice(h * HALF, (h + 1) * HALF)
-            for t in ts:
-                nc.vector.scalar_tensor_tensor(n[h][:, t, :], u[h][:, t, :], g_u[:, t : t + 1], y_g[:, t, cols], ALU.mult, ALU.add)
-
-        def add_turned(b, src, first, last):
+        def inverse_root(b):
+            nc.scalar.activation(rs_t[b][:], v_t[b][:], ACT.Abs_reciprocal_sqrt, bias=0.1)
+            rs[b] = psum.tile([P, PACK, BLOCK], F32, name="rs", tag="rs%d" % b)
             for t in range(PACK):
-                nc.tensor.matmul(v_t[b][:, t * P : (t + 1) * P], lhsT=src[:, t, :], rhs=ident[:], is_transpose=True,
-                                 start=(first and t == 0), stop=(last and t == PACK - 1))
-
-        def early_squares(h):
-            nc.scalar.activation(d_sq[h][:], d[h][:], ACT.Square, scale=SC_D)
-            for b in (2 * h, 2 * h + 1):
-                v_t[b] = psum.tile([P, PACK * P], F32, name="v_t", tag="acc", bufs=4)
-                add_turned(b, y_sq[:, :, b * BLOCK : (b + 1) * BLOCK], True, False)
-                add_turned(b, d_sq[h][:, :, (b % 2) * BLOCK : (b % 2 + 1) * BLOCK], False, False)
-
-        def late_squares(h):
-            for b in (2 * h, 2 * h + 1):
-                nc.scalar.activation(r_sq[b][:], r[h][:, :, (b % 2) * BLOCK : (b % 2 + 1) * BLOCK], ACT.Square, scale=SC_R)
-                add_turned(b, r_sq[b][:], False, True)
-
-        def inverse_roots(h):
-            for b in (2 * h, 2 * h + 1):
-                nc.scalar.activation(rs_t[b][:], v_t[b][:], ACT.Abs_reciprocal_sqrt, bias=0.1)
-                rs[b] = psum.tile([P, PACK, BLOCK], F32, name="rs", tag="rs", bufs=2)
-                for t in range(PACK):
-                    nc.tensor.transpose(rs[b][:, t, :], rs_t[b][:, t * P : (t + 1) * P], ident[:])
+                nc.tensor.transpose(rs[b][:, t, :], rs_t[b][:, t * P : (t + 1) * P], ident[:])
 
         z_bf = {}
 
         def scale_block(b):
             z_bf[b] = keep.tile([P, BLOCK * PACK], BF16, name="z_bf%d" % b, align_bytes=64)
-            n_b = n[b // 2][:, :, (b % 2) * BLOCK : (b % 2 + 1) * BLOCK]
+            n_b = n[:, :, b * BLOCK : (b + 1) * BLOCK]
             nc.vector.tensor_tensor(z_bf[b][:].rearrange("p (c i t) -> p c t i", i=4, t=PACK),
                                     rs[b][:].rearrange("p t (c i) -> p c t i", i=4),
                                     n_b.rearrange("p t (c i) -> p c t i", i=4), ALU.mult)
 
-        def finish_block(b):
+        def finish_block(b, parts):
             z_codes = keep.tile([P, BLOCK], U32, name="z_codes%d" % b, align_bytes=64)
             z_scales = keep.tile([P, BLOCK], U8, name="z_scales%d" % b, align_bytes=64)
             nc.vector.quantize_mx(out=z_codes[:].bitcast(FP8X4), scales=z_scales[:], in_=z_bf[b][:])
-            res = psum.tile([P, PACK * BLOCK], F32, name="res", tag="res", bufs=2)
-            for m in range(N // P):
-                rows = slice(m * P, (m + 1) * P)
-                nc.tensor.matmul_mx(out=res[:, m * BLOCK : (m + 1) * BLOCK], lhsT=w2_codes[:, rows].bitcast(FP8X4), lhsT_scale=w2_scales[:, rows],
-                                    rhs=z_codes[:].bitcast(FP8X4), rhs_scale=z_scales[:], start=True, stop=True)
-            staged = keep.tile([P, PACK * BLOCK], F32, name="staged%d" % b)
-            if b == 3:
-                nc.vector.tensor_copy(staged[:], res[:])
-            else:
-                nc.scalar.copy(staged[:], res[:])
-            nc.sync.dma_start(out.rearrange("(m p) j -> p m j", p=P)[:, :, b * BLOCK : (b + 1) * BLOCK], staged[:].rearrange("p (m j) -> p m j", m=PACK))
+            tiles = N // P // parts
+            for part in range(parts):
+                res = psum.tile([P, tiles, BLOCK], F32, name="res", tag="sum%d" % ((b + part) % 4))
+                for m in range(tiles):
+                    rows = slice((part * tiles + m) * P, (part * tiles + m + 1) * P)
+                    nc.tensor.matmul_mx(out=res[:, m, :], lhsT=w2_codes[:, rows].bitcast(FP8X4), lhsT_scale=w2_scales[:, rows],
+                                        rhs=z_codes[:].bitcast(FP8X4), rhs_scale=z_scales[:], start=True, stop=True)
+                staged = keep.tile([P, tiles, BLOCK], F32, name="staged%d_%d" % (b, part))
+                if part == 0:
+                    nc.scalar.copy(staged[:], res[:])
+                else:
+                    nc.vector.tensor_copy(staged[:], res[:])
+                rows = slice(part * tiles * P, (part + 1) * tiles * P)
+                queue = nc.scalar if parts == 2 and part == 0 else nc.sync
+                queue.dma_start(out[rows, b * BLOCK : (b + 1) * BLOCK].rearrange("(m p) j -> p m j", p=P), staged[:])
 
+        whole, left, right = slice(0, S), slice(0, HALF), slice(HALF, S)
         for t in range(PACK):
-            nc.scalar.activation(y_sq[:, t, :], y[t][:], ACT.Square, scale=SC_Y)
+            nc.scalar.activation(y_sq[:, t, :], y[t], ACT.Square, scale=SC_Y)
+        for b in range(4):
+            open_sum(b)
+        fetch_a(0, whole)
+        fetch_a(1, whole)
+        fetch_sum(0, whole)
+        fetch_sum(1, whole)
+        forms(0, whole)
         for t in range(PACK):
-            nc.scalar.activation(y_g[:, t, :], y[t][:], ACT.Copy, scale=g_y[:, t : t + 1])
-        gathers(0)
-        early_squares(0)
-        forms(0)
-        late_squares(0)
+            gain(t)
+        squares(0, whole)
+        fetch_a(2, whole)
+        forms(1, whole)
+        squares(1, whole)
         nc.scalar.copy(w2_bf[:].rearrange("p (c i j) -> p c j i", i=4, j=PACK), w2_raw[:].rearrange("p j (c i) -> p c j i", i=4))
-        inverse_roots(0)
-        gathers(1)
-        early_squares(1)
-        numerator(0, range(PACK))
-        nc.vector.quantize_mx(out=w2_codes[:].bitcast(FP8X4), scales=w2_scales[:], in_=w2_bf[:])
-        forms(1)
-        late_squares(1)
-        inverse_roots(1)
+        fetch_sum(2, whole)
+        fetch_a(3, whole)
+        forms(2, whole)
+        squares(2, whole)
+        fetch_sum(3, left)
+        fetch_sum(3, right)
+        forms(3, left)
+        squares(3, left)
+        forms(3, right)
+        squares(3, right)
+        for b in range(4):
+            inverse_root(b)
+        for t in range(PACK):
+            numerator(t, whole, whole)
         scale_block(0)
-        numerator(1, (0, 1))
-        finish_block(0)
+        nc.vector.quantize_mx(out=w2_codes[:].bitcast(FP8X4), scales=w2_scales[:], in_=w2_bf[:])
+        finish_block(0, 1)
         scale_block(1)
-        numerator(1, (2, 3))
-        finish_block(1)
         scale_block(2)
+        finish_block(1, 1)
+        finish_block(2, 1)
         scale_block(3)
-        finish_block(2)
-        finish_block(3)
+        finish_block(3, 2)

@@ -102,23 +102,23 @@ def tile_picked_zscore3_none_p_kernel(tc, x_words, x_scales, w1, gn, w2, offs, p
         y = [w[:, 0:S] for w in windows]
         for w in windows:
             nc.gpsimd.memset(w[:, S:], 0.0)
+        early = psum.tile([P, 2, HALF], F32, name="early", tag="sum3")
         for t in range(2):
-            early = psum.tile([P, HALF], F32, name="early", tag="rs%d" % t)
-            project(early[:], t, slice(0, HALF))
-            nc.vector.tensor_copy(y[t][:, 0:HALF], early[:])
+            project(early[:, t, :], t, slice(0, HALF))
+        for t in range(2):
+            nc.vector.tensor_copy(y[t][:, 0:HALF], early[:, t, :])
+        y_acc = []
         for t in range(PACK):
-            acc = psum.tile([P, S], F32, name="acc", tag="sum%d" % t)
+            acc = psum.tile([P, S], F32, name="acc", tag="rs%d" % t)
             cols = slice(HALF if t < 2 else 0, S)
             project(acc[:, cols], t, cols)
             nc.scalar.copy(y[t][:, cols], acc[:, cols])
+            y_acc.append(acc)
 
         y_sq = keep.tile([P, PACK, S], F32, name="y_sq")
         y_g = keep.tile([P, PACK, S], F32, name="y_g")
-        a = keep.tile([P, PACK, S], F32, name="a")
-        d = keep.tile([P, PACK, S], F32, name="d")
-        u = keep.tile([P, PACK, S], F32, name="u")
-        r = keep.tile([P, PACK, S], F32, name="r")
-        n = keep.tile([P, PACK, S], F32, name="n")
+        r_all = keep.tile([P, PACK, S], F32, name="r")
+        r = [r_all[:, t, :] for t in range(PACK)]
         d_sq = keep.tile([P, PACK, S], F32, name="d_sq")
         r_sq = keep.tile([P, PACK, S], F32, name="r_sq")
         rs_t = [keep.tile([P, PACK * P], F32, name="rs_t%d" % b) for b in range(4)]
@@ -128,19 +128,37 @@ def tile_picked_zscore3_none_p_kernel(tc, x_words, x_scales, w1, gn, w2, offs, p
         w2_codes = keep.tile([P, N], U32, name="w2_codes", align_bytes=64)
         w2_scales = keep.tile([P, N], U8, name="w2_scales", align_bytes=64)
 
-        def fetch_a(t, cols):
-            nc.vector.tensor_copy(a[:, t, cols], windows[t][:].indirect(p1_t[:, cols.start // 16 : cols.stop // 16]))
-
-        def fetch_sum(t, cols):
-            nc.vector.tensor_tensor(u[:, t, cols], windows[t][:].indirect(p2_t[:, cols.start // 16 : cols.stop // 16]), a[:, t, cols], ALU.add)
-
         def forms(t, cols):
-            nc.vector.scalar_tensor_tensor(d[:, t, cols], a[:, t, cols], -2.0, u[:, t, cols], ALU.mult, ALU.add)
-            nc.vector.scalar_tensor_tensor(r[:, t, cols], y[t][:, cols], LAM, u[:, t, cols], ALU.mult, ALU.add)
+            nc.vector.tensor_tensor(d[t][:, cols], a[t][:, cols], b_[t][:, cols], ALU.subtract)
+            nc.vector.scalar_tensor_tensor(r[t][:, cols], y[t][:, cols], LAM, u[t][:, cols], ALU.mult, ALU.add)
+
+        even = keep.tile([P, 2, S], F32, name="even")
+        odd = keep.tile([P, 1 + PACK, S], F32, name="odd")
+        a = [(even, odd)[t % 2][:, 1, :] for t in range(PACK)]
+        b_ = [(even, odd)[t % 2][:, 0, :] for t in range(PACK)]
+        u_own = keep.tile([P, PACK - 1, S], F32, name="u_own")
+        u = [u_own[:, t, :] for t in range(PACK - 1)] + [even[:, 0, :]]
+        d_own = keep.tile([P, PACK - 1, S], F32, name="d_own")
+        d = [d_own[:, t, :] for t in range(PACK - 1)] + [even[:, 1, :]]
+        n = odd[:, 1:, :].rearrange("p b (t j) -> p b t j", t=PACK)
+
+        def fetch_pair(t):
+            nc.vector.tensor_copy(a[t], windows[t][:].indirect(p1_t[:]))
+            nc.vector.tensor_copy(b_[t], windows[t][:].indirect(p2_t[:]))
+            if t < PACK - 1:
+                nc.gpsimd.tensor_tensor(u[t], a[t], b_[t], ALU.add)
+                nc.gpsimd.tensor_tensor(d[t], a[t], b_[t], ALU.subtract)
+
+        def form_r(t):
+            if t < 2:
+                nc.vector.scalar_tensor_tensor(r[t][:, 0:HALF], early[:, t, :], LAM, u[t][:, 0:HALF], ALU.mult, ALU.add)
+                nc.vector.scalar_tensor_tensor(r[t][:, HALF:], y_acc[t][:, HALF:], LAM, u[t][:, HALF:], ALU.mult, ALU.add)
+            else:
+                nc.vector.scalar_tensor_tensor(r[t], y_acc[t][:], LAM, u[t], ALU.mult, ALU.add)
 
         def squares(t, cols):
             for form, sq, scale in ((d, d_sq, SC_D), (r, r_sq, SC_R)):
-                nc.scalar.activation(sq[:, t, cols], form[:, t, cols], ACT.Square, scale=scale)
+                nc.scalar.activation(sq[:, t, cols], form[t][:, cols], ACT.Square, scale=scale)
                 for b in range(cols.start // BLOCK, cols.stop // BLOCK):
                     nc.tensor.matmul(v_t[b][:, t * P : (t + 1) * P], lhsT=sq[:, t, b * BLOCK : (b + 1) * BLOCK], rhs=ident[:],
                                      is_transpose=True, start=False, stop=form is r and t == PACK - 1)
@@ -148,8 +166,13 @@ def tile_picked_zscore3_none_p_kernel(tc, x_words, x_scales, w1, gn, w2, offs, p
         def gain(t):
             nc.scalar.activation(y_g[:, t, :], y[t], ACT.Copy, scale=g_y[:, t : t + 1])
 
-        def numerator(t, cols, place):
-            nc.vector.scalar_tensor_tensor(n[:, t, place], u[:, t, cols], g_u[:, t : t + 1], y_g[:, t, cols], ALU.mult, ALU.add)
+        def numerator(t):
+            nc.vector.scalar_tensor_tensor(n[:, :, t, :], u[t].rearrange("p (b j) -> p b j", j=BLOCK), g_u[:, t : t + 1],
+                                           y_g[:, t, :].rearrange("p (b j) -> p b j", j=BLOCK), ALU.mult, ALU.add)
+
+        def round_w2(cols):
+            nc.scalar.copy(w2_bf[:, cols.start * PACK : cols.stop * PACK].rearrange("p (c i j) -> p c j i", i=4, j=PACK),
+                           w2_raw[:, :, cols].rearrange("p j (c i) -> p c j i", i=4))
 
         def open_sum(b):
             v_t[b] = psum.tile([P, PACK * P], F32, name="v_t", tag="sum%d" % b)
@@ -167,7 +190,7 @@ def tile_picked_zscore3_none_p_kernel(tc, x_words, x_scales, w1, gn, w2, offs, p
 
         def scale_block(b):
             z_bf[b] = keep.tile([P, BLOCK * PACK], BF16, name="z_bf%d" % b, align_bytes=64)
-            n_b = n[:, :, b * BLOCK : (b + 1) * BLOCK]
+            n_b = n[:, b]
             nc.vector.tensor_tensor(z_bf[b][:].rearrange("p (c i t) -> p c t i", i=4, t=PACK),
                                     rs[b][:].rearrange("p t (c i) -> p c t i", i=4),
                                     n_b.rearrange("p t (c i) -> p c t i", i=4), ALU.mult)
@@ -195,26 +218,25 @@ def tile_picked_zscore3_none_p_kernel(tc, x_words, x_scales, w1, gn, w2, offs, p
         whole, left, right = slice(0, S), slice(0, HALF), slice(HALF, S)
         for t in range(PACK):
             nc.scalar.activation(y_sq[:, t, :], y[t], ACT.Square, scale=SC_Y)
-        for b in range(4):
+        for b in range(3):
             open_sum(b)
-        fetch_a(0, whole)
-        fetch_a(1, whole)
-        fetch_sum(0, whole)
-        fetch_sum(1, whole)
-        forms(0, whole)
+        fetch_pair(0)
+        fetch_pair(1)
+        form_r(0)
         for t in range(PACK):
             gain(t)
+        fetch_pair(2)
+        form_r(1)
+        open_sum(3)
         squares(0, whole)
-        fetch_a(2, whole)
-        forms(1, whole)
         squares(1, whole)
-        nc.scalar.copy(w2_bf[:].rearrange("p (c i j) -> p c j i", i=4, j=PACK), w2_raw[:].rearrange("p j (c i) -> p c j i", i=4))
-        fetch_sum(2, whole)
-        fetch_a(3, whole)
-        forms(2, whole)
+        round_w2(slice(0, 3 * P))
+        fetch_pair(3)
+        form_r(2)
         squares(2, whole)
-        fetch_sum(3, left)
-        fetch_sum(3, right)
+        round_w2(slice(3 * P, N))
+        for cols in (left, right):
+            nc.vector.tensor_tensor(u[3][:, cols], a[3][:, cols], b_[3][:, cols], ALU.add)
         forms(3, left)
         squares(3, left)
         forms(3, right)
@@ -222,7 +244,7 @@ def tile_picked_zscore3_none_p_kernel(tc, x_words, x_scales, w1, gn, w2, offs, p
         for b in range(4):
             inverse_root(b)
         for t in range(PACK):
-            numerator(t, whole, whole)
+            numerator(t)
         scale_block(0)
         nc.vector.quantize_mx(out=w2_codes[:].bitcast(FP8X4), scales=w2_scales[:], in_=w2_bf[:])
         finish_block(0, 1)

@@ -102,18 +102,18 @@ def tile_picked_zscore3_none_p_kernel(tc, x_words, x_scales, w1, gn, w2, offs, p
         y = [w[:, 0:S] for w in windows]
         for w in windows:
             nc.gpsimd.memset(w[:, S:], 0.0)
-        early = psum.tile([P, 2, HALF], F32, name="early", tag="sum3")
+        banks = [psum.tile([P, S], F32, name="y_bank", tag="rs%d" % e) for e in range(PACK)]
+        y_acc = {(t, h): banks[h][:, t * HALF : (t + 1) * HALF] for t in range(2) for h in range(2)}
         for t in range(2):
-            project(early[:, t, :], t, slice(0, HALF))
+            project(y_acc[t, 0], t, slice(0, HALF))
         for t in range(2):
-            nc.vector.tensor_copy(y[t][:, 0:HALF], early[:, t, :])
-        y_acc = []
-        for t in range(PACK):
-            acc = psum.tile([P, S], F32, name="acc", tag="rs%d" % t)
-            cols = slice(HALF if t < 2 else 0, S)
-            project(acc[:, cols], t, cols)
-            nc.scalar.copy(y[t][:, cols], acc[:, cols])
-            y_acc.append(acc)
+            nc.vector.tensor_copy(y[t][:, 0:HALF], y_acc[t, 0])
+        for t in range(2):
+            project(y_acc[t, 1], t, slice(HALF, S))
+            nc.scalar.copy(y[t][:, HALF:], y_acc[t, 1])
+        for t in range(2, PACK):
+            project(banks[t][:], t, slice(0, S))
+            nc.scalar.copy(y[t], banks[t][:])
 
         y_sq = keep.tile([P, PACK, S], F32, name="y_sq")
         y_g = keep.tile([P, PACK, S], F32, name="y_g")
@@ -129,7 +129,7 @@ def tile_picked_zscore3_none_p_kernel(tc, x_words, x_scales, w1, gn, w2, offs, p
         w2_scales = keep.tile([P, N], U8, name="w2_scales", align_bytes=64)
 
         def forms(t, cols):
-            nc.vector.tensor_tensor(d[t][:, cols], a[t][:, cols], b_[t][:, cols], ALU.subtract)
+            nc.vector.scalar_tensor_tensor(d[t][:, cols], a[t][:, cols], -2.0, u[t][:, cols], ALU.mult, ALU.add)
             nc.vector.scalar_tensor_tensor(r[t][:, cols], y[t][:, cols], LAM, u[t][:, cols], ALU.mult, ALU.add)
 
         even = keep.tile([P, 2, S], F32, name="even")
@@ -144,17 +144,19 @@ def tile_picked_zscore3_none_p_kernel(tc, x_words, x_scales, w1, gn, w2, offs, p
 
         def fetch_pair(t):
             nc.vector.tensor_copy(a[t], windows[t][:].indirect(p1_t[:]))
-            nc.vector.tensor_copy(b_[t], windows[t][:].indirect(p2_t[:]))
-            if t < PACK - 1:
+            if t == PACK - 1:
+                nc.vector.tensor_copy(b_[t][:, 0:HALF], windows[t][:].indirect(p2_t[:, 0 : HALF // 16]))
+            else:
+                nc.vector.tensor_copy(b_[t], windows[t][:].indirect(p2_t[:]))
                 nc.gpsimd.tensor_tensor(u[t], a[t], b_[t], ALU.add)
                 nc.gpsimd.tensor_tensor(d[t], a[t], b_[t], ALU.subtract)
 
         def form_r(t):
             if t < 2:
-                nc.vector.scalar_tensor_tensor(r[t][:, 0:HALF], early[:, t, :], LAM, u[t][:, 0:HALF], ALU.mult, ALU.add)
-                nc.vector.scalar_tensor_tensor(r[t][:, HALF:], y_acc[t][:, HALF:], LAM, u[t][:, HALF:], ALU.mult, ALU.add)
+                nc.vector.scalar_tensor_tensor(r[t][:, 0:HALF], y_acc[t, 0], LAM, u[t][:, 0:HALF], ALU.mult, ALU.add)
+                nc.vector.scalar_tensor_tensor(r[t][:, HALF:], y_acc[t, 1], LAM, u[t][:, HALF:], ALU.mult, ALU.add)
             else:
-                nc.vector.scalar_tensor_tensor(r[t], y_acc[t][:], LAM, u[t], ALU.mult, ALU.add)
+                nc.vector.scalar_tensor_tensor(r[t], banks[t][:], LAM, u[t], ALU.mult, ALU.add)
 
         def squares(t, cols):
             for form, sq, scale in ((d, d_sq, SC_D), (r, r_sq, SC_R)):
@@ -201,53 +203,53 @@ def tile_picked_zscore3_none_p_kernel(tc, x_words, x_scales, w1, gn, w2, offs, p
             nc.vector.quantize_mx(out=z_codes[:].bitcast(FP8X4), scales=z_scales[:], in_=z_bf[b][:])
             tiles = N // P // parts
             for part in range(parts):
-                res = psum.tile([P, tiles, BLOCK], F32, name="res", tag="sum%d" % ((b + part) % 4))
+                res = psum.tile([P, tiles, BLOCK], F32, name="res", tag="sum%d" % (part if parts == 2 else b + 1))
                 for m in range(tiles):
                     rows = slice((part * tiles + m) * P, (part * tiles + m + 1) * P)
                     nc.tensor.matmul_mx(out=res[:, m, :], lhsT=w2_codes[:, rows].bitcast(FP8X4), lhsT_scale=w2_scales[:, rows],
                                         rhs=z_codes[:].bitcast(FP8X4), rhs_scale=z_scales[:], start=True, stop=True)
                 staged = keep.tile([P, tiles, BLOCK], F32, name="staged%d_%d" % (b, part))
-                if part == 0:
+                if part == 0 or b == 0:
                     nc.scalar.copy(staged[:], res[:])
                 else:
                     nc.vector.tensor_copy(staged[:], res[:])
                 rows = slice(part * tiles * P, (part + 1) * tiles * P)
-                queue = nc.scalar if parts == 2 and part == 0 else nc.sync
+                queue = nc.scalar if b == 3 and part == 0 else nc.sync
                 queue.dma_start(out[rows, b * BLOCK : (b + 1) * BLOCK].rearrange("(m p) j -> p m j", p=P), staged[:])
 
         whole, left, right = slice(0, S), slice(0, HALF), slice(HALF, S)
         for t in range(PACK):
             nc.scalar.activation(y_sq[:, t, :], y[t], ACT.Square, scale=SC_Y)
-        for b in range(3):
+        for b in range(4):
             open_sum(b)
+        for t in range(PACK):
+            gain(t)
         fetch_pair(0)
         fetch_pair(1)
         form_r(0)
-        for t in range(PACK):
-            gain(t)
         fetch_pair(2)
         form_r(1)
-        open_sum(3)
         squares(0, whole)
+        round_w2(slice(0, P))
         squares(1, whole)
-        round_w2(slice(0, 3 * P))
+        round_w2(slice(P, N - 64))
         fetch_pair(3)
         form_r(2)
         squares(2, whole)
-        round_w2(slice(3 * P, N))
-        for cols in (left, right):
-            nc.vector.tensor_tensor(u[3][:, cols], a[3][:, cols], b_[3][:, cols], ALU.add)
+        nc.vector.tensor_tensor(u[3][:, left], a[3][:, left], b_[3][:, left], ALU.add)
+        nc.vector.tensor_tensor(u[3][:, right], windows[3][:].indirect(p2_t[:, HALF // 16 :]), a[3][:, right], ALU.add)
         forms(3, left)
         squares(3, left)
         forms(3, right)
         squares(3, right)
+        round_w2(slice(N - 64, N))
         for b in range(4):
             inverse_root(b)
         for t in range(PACK):
             numerator(t)
         scale_block(0)
         nc.vector.quantize_mx(out=w2_codes[:].bitcast(FP8X4), scales=w2_scales[:], in_=w2_bf[:])
-        finish_block(0, 1)
+        finish_block(0, 2)
         scale_block(1)
         scale_block(2)
         finish_block(1, 1)

@@ -1,5 +1,5 @@
-from contextlib import ExitStack
 import math
+from contextlib import ExitStack
 
 import concourse.mybir as mybir
 from concourse.masks import make_identity
@@ -19,17 +19,32 @@ ACT = mybir.ActivationFunctionType
 
 P = 128
 PACK = 4
+LAST = PACK - 1
+GROUP = 16
 BLOCK = 128
-HALF = 256
+BLOCKS = S // BLOCK
+HALF = S // 2
+RUN = 4
+W2_TAIL = 64
+WHOLE, LEFT, RIGHT = slice(0, S), slice(0, HALF), slice(HALF, S)
 
 C_MU = 0.3125
-K_S = 2 * C_MU - 3 * C_MU * C_MU
-A_R = 0.5 - K_S
-LAM = -K_S / A_R
-B_Y = (1 - K_S) - K_S * K_S / A_R
-SC_D = math.sqrt(0.25 * 0.5)
-SC_R = math.sqrt(0.25 * A_R)
-SC_Y = math.sqrt(0.25 * B_Y)
+K_SUM = 2 * C_MU - 3 * C_MU * C_MU
+A_R = 0.5 - K_SUM
+LAM = -K_SUM / A_R
+B_Y = (1 - K_SUM) - K_SUM * K_SUM / A_R
+D_INVERSE_WEIGHT = 8.0
+SCALE_R = math.sqrt(0.25 * A_R)
+SCALE_Y = math.sqrt(0.25 * B_Y)
+EPS = 0.1
+
+
+def entries(cols):
+    return slice(cols.start // GROUP, cols.stop // GROUP)
+
+
+def block(b):
+    return slice(b * BLOCK, (b + 1) * BLOCK)
 
 
 def tile_picked_zscore3_none_p_kernel(tc, x_words, x_scales, w1, gn, w2, offs, p1, p2, out):
@@ -38,9 +53,9 @@ def tile_picked_zscore3_none_p_kernel(tc, x_words, x_scales, w1, gn, w2, offs, p
         keep = ctx.enter_context(tc.tile_pool(name="keep", bufs=1))
         psum = ctx.enter_context(tc.psum_pool(name="psum", bufs=1))
 
-        offs_t = keep.tile([P, S // 16], U16, name="offs_t")
-        p1_t = keep.tile([P, S // 16], U16, name="p1_t")
-        p2_t = keep.tile([P, S // 16], U16, name="p2_t")
+        offs_t = keep.tile([P, S // GROUP], U16, name="offs_t")
+        p1_t = keep.tile([P, S // GROUP], U16, name="p1_t")
+        p2_t = keep.tile([P, S // GROUP], U16, name="p2_t")
         xs_all = keep.tile([P, T], U8, name="xs_all")
         xw_all = keep.tile([P, T], U32, name="xw_all")
         w1_raw = keep.tile([P, PACK, H], F32, name="w1_raw")
@@ -50,17 +65,18 @@ def tile_picked_zscore3_none_p_kernel(tc, x_words, x_scales, w1, gn, w2, offs, p
         nc.gpsimd.memset(xs_all[:].bitcast(I32), 0)
         nc.sync.dma_start(offs_t[:], offs)
         nc.sync.dma_start(w1_raw[:], w1.rearrange("(p j) c -> p j c", j=PACK))
-        for q in range(4):
-            nc.sync.dma_start(xs_all[q:P:32, :].bitcast(I32), x_scales[0, q:16:4, :].bitcast(I32))
+        for row in range(4):
+            nc.sync.dma_start(xs_all[row:P:32, :].bitcast(I32), x_scales[0, row:16:4, :].bitcast(I32))
         nc.sync.dma_start(xw_all[:].bitcast(I32), x_words[0].rearrange("p n t -> p (n t)").bitcast(I32))
         nc.sync.dma_start(p1_t[:], p1)
         nc.sync.dma_start(p2_t[:], p2)
         nc.sync.dma_start(gn_t[:], gn.rearrange("(p t) o -> p (t o)", t=PACK))
         nc.sync.dma_start(w2_raw[:], w2.rearrange("(p j) c -> p j c", j=PACK))
 
-        warm = keep.tile([P, 2], F32, name="warm")
-        nc.vector.memset(warm[:, 0:1], 1.0)
-        nc.scalar.activation(warm[:, 1:2], warm[:, 0:1], ACT.Abs_reciprocal_sqrt)
+        d_weight = keep.tile([P, 2], F32, name="d_weight")
+        nc.vector.memset(d_weight[:, 0:1], D_INVERSE_WEIGHT)
+        nc.scalar.activation(d_weight[:, 1:2], d_weight[:, 0:1], ACT.Abs_reciprocal_sqrt)
+        scale_d = d_weight[:, 1:2]
 
         ident = keep.tile([P, P], F32, name="ident")
         make_identity(nc, ident[:])
@@ -70,28 +86,22 @@ def tile_picked_zscore3_none_p_kernel(tc, x_words, x_scales, w1, gn, w2, offs, p
         nc.vector.tensor_copy(xs[:], xs_all[:].indirect(offs_t[:]))
 
         w1_src = w1_raw[:].rearrange("p j (m t) -> p m j t", t=PACK)
-        w1_codes, w1_scales = [], []
-        w1_bf = []
-        for h in range(2):
-            b = keep.tile([P, 2 * P * PACK], BF16, name="w1_bf%d" % h, align_bytes=64)
-            dst = b[:].rearrange("p (t m j) -> p m j t", t=2, j=PACK)
-            if h == 0:
-                nc.vector.tensor_copy(dst, w1_src[:, :, :, 0:2])
-            else:
-                nc.scalar.copy(dst, w1_src[:, :, :, 2:4])
-            w1_bf.append(b)
-        for h in range(2):
-            c = keep.tile([P, 2 * P], U32, name="w1_c%d" % h, align_bytes=64)
-            s = keep.tile([P, 2 * P], U8, name="w1_s%d" % h, align_bytes=64)
-            nc.vector.quantize_mx(out=c[:].bitcast(FP8X4), scales=s[:], in_=w1_bf[h][:])
-            w1_codes.append(c)
-            w1_scales.append(s)
-        g_u = keep.tile([P, PACK], F32, name="g_u")
-        g_y = keep.tile([P, PACK], F32, name="g_y")
-        nc.scalar.activation(g_u[:], gn_t[:], ACT.Copy, scale=-C_MU)
-        nc.scalar.activation(g_y[:], gn_t[:], ACT.Copy, scale=1 - C_MU)
-        for h in range(2):
-            nc.vector.tensor_copy(xw[:, h * HALF : (h + 1) * HALF], xw_all[:].indirect(offs_t[:, h * HALF // 16 : (h + 1) * HALF // 16]))
+        w1_bf, w1_codes, w1_scales = [], [], []
+        for pair, round_copy in enumerate((nc.vector.tensor_copy, nc.scalar.copy)):
+            w1_bf.append(keep.tile([P, 2 * P * PACK], BF16, name="w1_bf%d" % pair, align_bytes=64))
+            round_copy(w1_bf[pair][:].rearrange("p (t m j) -> p m j t", t=2, j=PACK), w1_src[:, :, :, 2 * pair : 2 * pair + 2])
+        for pair in range(2):
+            w1_codes.append(keep.tile([P, 2 * P], U32, name="w1_c%d" % pair, align_bytes=64))
+            w1_scales.append(keep.tile([P, 2 * P], U8, name="w1_s%d" % pair, align_bytes=64))
+            nc.vector.quantize_mx(out=w1_codes[pair][:].bitcast(FP8X4), scales=w1_scales[pair][:], in_=w1_bf[pair][:])
+
+        gain_u = keep.tile([P, PACK], F32, name="gain_u")
+        gain_y = keep.tile([P, PACK], F32, name="gain_y")
+        nc.scalar.activation(gain_u[:], gn_t[:], ACT.Copy, scale=-C_MU)
+        nc.scalar.activation(gain_y[:], gn_t[:], ACT.Copy, scale=1 - C_MU)
+
+        for cols in (LEFT, RIGHT):
+            nc.vector.tensor_copy(xw[:, cols], xw_all[:].indirect(offs_t[:, entries(cols)]))
 
         def project(dst, t, cols):
             w = slice((t % 2) * P, (t % 2 + 1) * P)
@@ -102,157 +112,146 @@ def tile_picked_zscore3_none_p_kernel(tc, x_words, x_scales, w1, gn, w2, offs, p
         y = [w[:, 0:S] for w in windows]
         for w in windows:
             nc.gpsimd.memset(w[:, S:], 0.0)
+
         banks = [psum.tile([P, S], F32, name="y_bank", tag="rs%d" % e) for e in range(PACK)]
-        y_acc = {(t, h): banks[h][:, t * HALF : (t + 1) * HALF] for t in range(2) for h in range(2)}
+        y_half = {(t, h): banks[h][:, t * HALF : (t + 1) * HALF] for t in range(2) for h in range(2)}
         for t in range(2):
-            project(y_acc[t, 0], t, slice(0, HALF))
+            project(y_half[t, 0], t, LEFT)
         for t in range(2):
-            nc.vector.tensor_copy(y[t][:, 0:HALF], y_acc[t, 0])
+            nc.vector.tensor_copy(y[t][:, LEFT], y_half[t, 0])
         for t in range(2):
-            project(y_acc[t, 1], t, slice(HALF, S))
-            nc.scalar.copy(y[t][:, HALF:], y_acc[t, 1])
+            project(y_half[t, 1], t, RIGHT)
+            nc.scalar.copy(y[t][:, RIGHT], y_half[t, 1])
         for t in range(2, PACK):
-            project(banks[t][:], t, slice(0, S))
+            project(banks[t][:], t, WHOLE)
             nc.scalar.copy(y[t], banks[t][:])
 
         y_sq = keep.tile([P, PACK, S], F32, name="y_sq")
-        y_g = keep.tile([P, PACK, S], F32, name="y_g")
-        r_all = keep.tile([P, PACK, S], F32, name="r")
-        r = [r_all[:, t, :] for t in range(PACK)]
+        y_gained = keep.tile([P, PACK, S], F32, name="y_gained")
+        r_all = keep.tile([P, PACK, S], F32, name="r_all")
         d_sq = keep.tile([P, PACK, S], F32, name="d_sq")
         r_sq = keep.tile([P, PACK, S], F32, name="r_sq")
-        rs_t = [keep.tile([P, PACK * P], F32, name="rs_t%d" % b) for b in range(4)]
-        v_t = {}
-        rs = {}
+        roots_turned = [keep.tile([P, PACK * P], F32, name="roots_turned%d" % b) for b in range(BLOCKS)]
         w2_bf = keep.tile([P, N * PACK], BF16, name="w2_bf", align_bytes=64)
         w2_codes = keep.tile([P, N], U32, name="w2_codes", align_bytes=64)
         w2_scales = keep.tile([P, N], U8, name="w2_scales", align_bytes=64)
 
-        def forms(t, cols):
-            nc.vector.scalar_tensor_tensor(d[t][:, cols], a[t][:, cols], -2.0, u[t][:, cols], ALU.mult, ALU.add)
-            nc.vector.scalar_tensor_tensor(r[t][:, cols], y[t][:, cols], LAM, u[t][:, cols], ALU.mult, ALU.add)
-
         even = keep.tile([P, 2, S], F32, name="even")
-        odd = keep.tile([P, 1 + PACK, S], F32, name="odd")
+        odd = keep.tile([P, 1 + BLOCKS, S], F32, name="odd")
+        u_own = keep.tile([P, LAST, S], F32, name="u_own")
+        d_own = keep.tile([P, LAST, S], F32, name="d_own")
         a = [(even, odd)[t % 2][:, 1, :] for t in range(PACK)]
-        b_ = [(even, odd)[t % 2][:, 0, :] for t in range(PACK)]
-        u_own = keep.tile([P, PACK - 1, S], F32, name="u_own")
-        u = [u_own[:, t, :] for t in range(PACK - 1)] + [even[:, 0, :]]
-        d_own = keep.tile([P, PACK - 1, S], F32, name="d_own")
-        d = [d_own[:, t, :] for t in range(PACK - 1)] + [even[:, 1, :]]
-        n = odd[:, 1:, :].rearrange("p b (t j) -> p b t j", t=PACK)
+        b = [(even, odd)[t % 2][:, 0, :] for t in range(PACK)]
+        u = [u_own[:, t, :] for t in range(LAST)] + [even[:, 0, :]]
+        d = [d_own[:, t, :] for t in range(LAST)] + [even[:, 1, :]]
+        r = [r_all[:, t, :] for t in range(PACK)]
+        numerators = odd[:, 1:, :].rearrange("p n (c t i) -> p n c t i", t=PACK, i=RUN)
+        sums, roots, z_bf = {}, {}, {}
 
-        def fetch_pair(t):
-            nc.vector.tensor_copy(a[t], windows[t][:].indirect(p1_t[:]))
-            if t == PACK - 1:
-                nc.vector.tensor_copy(b_[t][:, 0:HALF], windows[t][:].indirect(p2_t[:, 0 : HALF // 16]))
-            else:
-                nc.vector.tensor_copy(b_[t], windows[t][:].indirect(p2_t[:]))
-                nc.gpsimd.tensor_tensor(u[t], a[t], b_[t], ALU.add)
-                nc.gpsimd.tensor_tensor(d[t], a[t], b_[t], ALU.subtract)
+        def fetch(t, cols):
+            nc.vector.tensor_copy(a[t][:, cols], windows[t][:].indirect(p1_t[:, entries(cols)]))
+            nc.vector.tensor_copy(b[t][:, cols], windows[t][:].indirect(p2_t[:, entries(cols)]))
+            if t < LAST:
+                nc.gpsimd.tensor_tensor(u[t][:, cols], a[t][:, cols], b[t][:, cols], ALU.add)
+                nc.gpsimd.tensor_tensor(d[t][:, cols], a[t][:, cols], b[t][:, cols], ALU.subtract)
 
-        def form_r(t):
+        def form_r(t, cols, y_part):
+            nc.vector.scalar_tensor_tensor(r[t][:, cols], y_part, LAM, u[t][:, cols], ALU.mult, ALU.add)
+
+        def form_r_beside_gpsimd(t):
             if t < 2:
-                nc.vector.scalar_tensor_tensor(r[t][:, 0:HALF], y_acc[t, 0], LAM, u[t][:, 0:HALF], ALU.mult, ALU.add)
-                nc.vector.scalar_tensor_tensor(r[t][:, HALF:], y_acc[t, 1], LAM, u[t][:, HALF:], ALU.mult, ALU.add)
+                form_r(t, LEFT, y_half[t, 0])
+                form_r(t, RIGHT, y_half[t, 1])
             else:
-                nc.vector.scalar_tensor_tensor(r[t], banks[t][:], LAM, u[t], ALU.mult, ALU.add)
+                form_r(t, WHOLE, banks[t][:])
 
-        def squares(t, cols):
-            for form, sq, scale in ((d, d_sq, SC_D), (r, r_sq, SC_R)):
-                nc.scalar.activation(sq[:, t, cols], form[t][:, cols], ACT.Square, scale=scale)
-                for b in range(cols.start // BLOCK, cols.stop // BLOCK):
-                    nc.tensor.matmul(v_t[b][:, t * P : (t + 1) * P], lhsT=sq[:, t, b * BLOCK : (b + 1) * BLOCK], rhs=ident[:],
-                                     is_transpose=True, start=False, stop=form is r and t == PACK - 1)
+        def add_turned(squares, t, n, start, stop):
+            nc.tensor.matmul(sums[n][:, t * P : (t + 1) * P], lhsT=squares[:, t, block(n)], rhs=ident[:],
+                             is_transpose=True, start=start, stop=stop)
 
-        def gain(t):
-            nc.scalar.activation(y_g[:, t, :], y[t], ACT.Copy, scale=g_y[:, t : t + 1])
-
-        def numerator(t):
-            nc.vector.scalar_tensor_tensor(n[:, :, t, :], u[t].rearrange("p (b j) -> p b j", j=BLOCK), g_u[:, t : t + 1],
-                                           y_g[:, t, :].rearrange("p (b j) -> p b j", j=BLOCK), ALU.mult, ALU.add)
+        def add_squares(t, cols):
+            for form, squares, scale in ((d, d_sq, scale_d), (r, r_sq, SCALE_R)):
+                nc.scalar.activation(squares[:, t, cols], form[t][:, cols], ACT.Square, scale=scale)
+                for n in range(cols.start // BLOCK, cols.stop // BLOCK):
+                    add_turned(squares, t, n, False, form is r and t == LAST)
 
         def round_w2(cols):
-            nc.scalar.copy(w2_bf[:, cols.start * PACK : cols.stop * PACK].rearrange("p (c i j) -> p c j i", i=4, j=PACK),
-                           w2_raw[:, :, cols].rearrange("p j (c i) -> p c j i", i=4))
+            nc.scalar.copy(w2_bf[:, cols.start * PACK : cols.stop * PACK].rearrange("p (c i j) -> p c j i", i=RUN, j=PACK),
+                           w2_raw[:, :, cols].rearrange("p j (c i) -> p c j i", i=RUN))
 
-        def open_sum(b):
-            v_t[b] = psum.tile([P, PACK * P], F32, name="v_t", tag="sum%d" % b)
+        def inverse_root(n):
+            nc.scalar.activation(roots_turned[n][:], sums[n][:], ACT.Abs_reciprocal_sqrt, bias=EPS)
+            roots[n] = psum.tile([P, PACK, BLOCK], F32, name="roots", tag="rs%d" % n)
             for t in range(PACK):
-                nc.tensor.matmul(v_t[b][:, t * P : (t + 1) * P], lhsT=y_sq[:, t, b * BLOCK : (b + 1) * BLOCK], rhs=ident[:],
-                                 is_transpose=True, start=t == 0, stop=False)
+                nc.tensor.transpose(roots[n][:, t, :], roots_turned[n][:, t * P : (t + 1) * P], ident[:])
 
-        def inverse_root(b):
-            nc.scalar.activation(rs_t[b][:], v_t[b][:], ACT.Abs_reciprocal_sqrt, bias=0.1)
-            rs[b] = psum.tile([P, PACK, BLOCK], F32, name="rs", tag="rs%d" % b)
-            for t in range(PACK):
-                nc.tensor.transpose(rs[b][:, t, :], rs_t[b][:, t * P : (t + 1) * P], ident[:])
+        def numerator(t):
+            nc.vector.scalar_tensor_tensor(numerators[:, :, :, t, :].rearrange("p n c i -> p (n c) i"),
+                                           u[t].rearrange("p (c i) -> p c i", i=RUN), gain_u[:, t : t + 1],
+                                           y_gained[:, t, :].rearrange("p (c i) -> p c i", i=RUN), ALU.mult, ALU.add)
 
-        z_bf = {}
+        def form_z(n):
+            z_bf[n] = keep.tile([P, BLOCK * PACK], BF16, name="z_bf%d" % n, align_bytes=64)
+            nc.vector.tensor_tensor(z_bf[n][:].rearrange("p (c i t) -> p c t i", i=RUN, t=PACK),
+                                    roots[n][:].rearrange("p t (c i) -> p c t i", i=RUN), numerators[:, n], ALU.mult)
 
-        def scale_block(b):
-            z_bf[b] = keep.tile([P, BLOCK * PACK], BF16, name="z_bf%d" % b, align_bytes=64)
-            n_b = n[:, b]
-            nc.vector.tensor_tensor(z_bf[b][:].rearrange("p (c i t) -> p c t i", i=4, t=PACK),
-                                    rs[b][:].rearrange("p t (c i) -> p c t i", i=4),
-                                    n_b.rearrange("p t (c i) -> p c t i", i=4), ALU.mult)
-
-        def finish_block(b, parts):
-            z_codes = keep.tile([P, BLOCK], U32, name="z_codes%d" % b, align_bytes=64)
-            z_scales = keep.tile([P, BLOCK], U8, name="z_scales%d" % b, align_bytes=64)
-            nc.vector.quantize_mx(out=z_codes[:].bitcast(FP8X4), scales=z_scales[:], in_=z_bf[b][:])
-            tiles = N // P // parts
-            for part in range(parts):
-                res = psum.tile([P, tiles, BLOCK], F32, name="res", tag="sum%d" % (part if parts == 2 else b + 1))
+        def second_product(n, parts):
+            z_codes = keep.tile([P, BLOCK], U32, name="z_codes%d" % n, align_bytes=64)
+            z_scales = keep.tile([P, BLOCK], U8, name="z_scales%d" % n, align_bytes=64)
+            nc.vector.quantize_mx(out=z_codes[:].bitcast(FP8X4), scales=z_scales[:], in_=z_bf[n][:])
+            tiles = N // P // len(parts)
+            for part, (bank, copy_out, queue) in enumerate(parts):
+                result = psum.tile([P, tiles, BLOCK], F32, name="result", tag=bank)
                 for m in range(tiles):
-                    rows = slice((part * tiles + m) * P, (part * tiles + m + 1) * P)
-                    nc.tensor.matmul_mx(out=res[:, m, :], lhsT=w2_codes[:, rows].bitcast(FP8X4), lhsT_scale=w2_scales[:, rows],
+                    w = slice((part * tiles + m) * P, (part * tiles + m + 1) * P)
+                    nc.tensor.matmul_mx(out=result[:, m, :], lhsT=w2_codes[:, w].bitcast(FP8X4), lhsT_scale=w2_scales[:, w],
                                         rhs=z_codes[:].bitcast(FP8X4), rhs_scale=z_scales[:], start=True, stop=True)
-                staged = keep.tile([P, tiles, BLOCK], F32, name="staged%d_%d" % (b, part))
-                if part == 0 or b == 0:
-                    nc.scalar.copy(staged[:], res[:])
-                else:
-                    nc.vector.tensor_copy(staged[:], res[:])
+                staged = keep.tile([P, tiles, BLOCK], F32, name="staged%d_%d" % (n, part))
+                copy_out(staged[:], result[:])
                 rows = slice(part * tiles * P, (part + 1) * tiles * P)
-                queue = nc.scalar if b == 3 and part == 0 else nc.sync
-                queue.dma_start(out[rows, b * BLOCK : (b + 1) * BLOCK].rearrange("(m p) j -> p m j", p=P), staged[:])
+                queue.dma_start(out[rows, block(n)].rearrange("(m p) j -> p m j", p=P), staged[:])
 
-        whole, left, right = slice(0, S), slice(0, HALF), slice(HALF, S)
         for t in range(PACK):
-            nc.scalar.activation(y_sq[:, t, :], y[t], ACT.Square, scale=SC_Y)
-        for b in range(4):
-            open_sum(b)
+            nc.scalar.activation(y_sq[:, t, :], y[t], ACT.Square, scale=SCALE_Y)
+        for n in range(BLOCKS):
+            sums[n] = psum.tile([P, PACK * P], F32, name="sums", tag="sum%d" % n)
+            for t in range(PACK):
+                add_turned(y_sq, t, n, t == 0, False)
         for t in range(PACK):
-            gain(t)
-        fetch_pair(0)
-        fetch_pair(1)
-        form_r(0)
-        fetch_pair(2)
-        form_r(1)
-        squares(0, whole)
+            nc.scalar.activation(y_gained[:, t, :], y[t], ACT.Copy, scale=gain_y[:, t : t + 1])
+
+        fetch(0, LEFT)
+        fetch(0, RIGHT)
+        fetch(1, WHOLE)
+        form_r_beside_gpsimd(0)
+        fetch(2, WHOLE)
+        form_r_beside_gpsimd(1)
+        add_squares(0, WHOLE)
         round_w2(slice(0, P))
-        squares(1, whole)
-        round_w2(slice(P, N - 64))
-        fetch_pair(3)
-        form_r(2)
-        squares(2, whole)
-        nc.vector.tensor_tensor(u[3][:, left], a[3][:, left], b_[3][:, left], ALU.add)
-        nc.vector.tensor_tensor(u[3][:, right], windows[3][:].indirect(p2_t[:, HALF // 16 :]), a[3][:, right], ALU.add)
-        forms(3, left)
-        squares(3, left)
-        forms(3, right)
-        squares(3, right)
-        round_w2(slice(N - 64, N))
-        for b in range(4):
-            inverse_root(b)
+        add_squares(1, WHOLE)
+        round_w2(slice(P, N - W2_TAIL))
+        fetch(LAST, WHOLE)
+        form_r_beside_gpsimd(2)
+        add_squares(2, WHOLE)
+
+        for cols in (LEFT, RIGHT):
+            nc.vector.tensor_tensor(u[LAST][:, cols], a[LAST][:, cols], b[LAST][:, cols], ALU.add)
+        for cols in (LEFT, RIGHT):
+            nc.vector.scalar_tensor_tensor(d[LAST][:, cols], a[LAST][:, cols], -2.0, u[LAST][:, cols], ALU.mult, ALU.add)
+            form_r(LAST, cols, y[LAST][:, cols])
+            add_squares(LAST, cols)
+        round_w2(slice(N - W2_TAIL, N))
+        for n in range(BLOCKS):
+            inverse_root(n)
         for t in range(PACK):
             numerator(t)
-        scale_block(0)
+
+        form_z(0)
         nc.vector.quantize_mx(out=w2_codes[:].bitcast(FP8X4), scales=w2_scales[:], in_=w2_bf[:])
-        finish_block(0, 2)
-        scale_block(1)
-        scale_block(2)
-        finish_block(1, 1)
-        finish_block(2, 1)
-        scale_block(3)
-        finish_block(3, 2)
+        second_product(0, (("sum0", nc.scalar.copy, nc.sync), ("sum1", nc.scalar.copy, nc.sync)))
+        form_z(1)
+        form_z(2)
+        second_product(1, (("sum2", nc.scalar.copy, nc.sync),))
+        second_product(2, (("sum3", nc.scalar.copy, nc.sync),))
+        form_z(3)
+        second_product(3, (("sum0", nc.scalar.copy, nc.scalar), ("sum1", nc.vector.tensor_copy, nc.sync)))

import math
from contextlib import ExitStack

import concourse.mybir as mybir
from concourse.masks import make_identity

K, T, S, N, H = 512, 2048, 512, 512, 512
FLOPS = 2 * K * H * S + 2 * H * N * S

F32 = mybir.dt.float32
BF16 = mybir.dt.bfloat16
U32 = mybir.dt.uint32
I32 = mybir.dt.int32
U16 = mybir.dt.uint16
U8 = mybir.dt.uint8
FP8X4 = mybir.dt.float8_e4m3fn_x4
ALU = mybir.AluOpType
ACT = mybir.ActivationFunctionType

P = 128
PACK = 4
LAST = PACK - 1
GROUP = 16
BLOCK = 128
BLOCKS = S // BLOCK
HALF = S // 2
RUN = 4
W2_TAIL = 64
WHOLE, LEFT, RIGHT = slice(0, S), slice(0, HALF), slice(HALF, S)

C_MU = 0.3125
K_SUM = 2 * C_MU - 3 * C_MU * C_MU
A_R = 0.5 - K_SUM
LAM = -K_SUM / A_R
B_Y = (1 - K_SUM) - K_SUM * K_SUM / A_R
D_INVERSE_WEIGHT = 8.0
SCALE_R = math.sqrt(0.25 * A_R)
SCALE_Y = math.sqrt(0.25 * B_Y)
EPS = 0.1


def entries(cols):
    return slice(cols.start // GROUP, cols.stop // GROUP)


def block(b):
    return slice(b * BLOCK, (b + 1) * BLOCK)


def tile_picked_zscore3_none_p_kernel(tc, x_words, x_scales, w1, gn, w2, offs, p1, p2, out):
    nc = tc.nc
    with ExitStack() as ctx:
        keep = ctx.enter_context(tc.tile_pool(name="keep", bufs=1))
        psum = ctx.enter_context(tc.psum_pool(name="psum", bufs=1))

        offs_t = keep.tile([P, S // GROUP], U16, name="offs_t")
        p1_t = keep.tile([P, S // GROUP], U16, name="p1_t")
        p2_t = keep.tile([P, S // GROUP], U16, name="p2_t")
        xs_all = keep.tile([P, T], U8, name="xs_all")
        xw_all = keep.tile([P, T], U32, name="xw_all")
        w1_raw = keep.tile([P, PACK, H], F32, name="w1_raw")
        w2_raw = keep.tile([P, PACK, N], F32, name="w2_raw")
        gn_t = keep.tile([P, PACK], F32, name="gn_t")

        nc.gpsimd.memset(xs_all[:].bitcast(I32), 0)
        nc.sync.dma_start(offs_t[:], offs)
        nc.sync.dma_start(w1_raw[:], w1.rearrange("(p j) c -> p j c", j=PACK))
        for row in range(4):
            nc.sync.dma_start(xs_all[row:P:32, :].bitcast(I32), x_scales[0, row:16:4, :].bitcast(I32))
        nc.sync.dma_start(xw_all[:].bitcast(I32), x_words[0].rearrange("p n t -> p (n t)").bitcast(I32))
        nc.sync.dma_start(p1_t[:], p1)
        nc.sync.dma_start(p2_t[:], p2)
        nc.sync.dma_start(gn_t[:], gn.rearrange("(p t) o -> p (t o)", t=PACK))
        nc.sync.dma_start(w2_raw[:], w2.rearrange("(p j) c -> p j c", j=PACK))

        d_weight = keep.tile([P, 2], F32, name="d_weight")
        nc.vector.memset(d_weight[:, 0:1], D_INVERSE_WEIGHT)
        nc.scalar.activation(d_weight[:, 1:2], d_weight[:, 0:1], ACT.Abs_reciprocal_sqrt)
        scale_d = d_weight[:, 1:2]

        ident = keep.tile([P, P], F32, name="ident")
        make_identity(nc, ident[:])

        xs = keep.tile([P, S], U8, name="xs", align_bytes=64)
        xw = keep.tile([P, S], U32, name="xw", align_bytes=64)
        nc.vector.tensor_copy(xs[:], xs_all[:].indirect(offs_t[:]))

        w1_src = w1_raw[:].rearrange("p j (m t) -> p m j t", t=PACK)
        w1_bf, w1_codes, w1_scales = [], [], []
        for pair, round_copy in enumerate((nc.vector.tensor_copy, nc.scalar.copy)):
            w1_bf.append(keep.tile([P, 2 * P * PACK], BF16, name="w1_bf%d" % pair, align_bytes=64))
            round_copy(w1_bf[pair][:].rearrange("p (t m j) -> p m j t", t=2, j=PACK), w1_src[:, :, :, 2 * pair : 2 * pair + 2])
        for pair in range(2):
            w1_codes.append(keep.tile([P, 2 * P], U32, name="w1_c%d" % pair, align_bytes=64))
            w1_scales.append(keep.tile([P, 2 * P], U8, name="w1_s%d" % pair, align_bytes=64))
            nc.vector.quantize_mx(out=w1_codes[pair][:].bitcast(FP8X4), scales=w1_scales[pair][:], in_=w1_bf[pair][:])

        gain_u = keep.tile([P, PACK], F32, name="gain_u")
        gain_y = keep.tile([P, PACK], F32, name="gain_y")
        nc.scalar.activation(gain_u[:], gn_t[:], ACT.Copy, scale=-C_MU)
        nc.scalar.activation(gain_y[:], gn_t[:], ACT.Copy, scale=1 - C_MU)

        for cols in (LEFT, RIGHT):
            nc.vector.tensor_copy(xw[:, cols], xw_all[:].indirect(offs_t[:, entries(cols)]))

        def project(dst, t, cols):
            w = slice((t % 2) * P, (t % 2 + 1) * P)
            nc.tensor.matmul_mx(out=dst, lhsT=w1_codes[t // 2][:, w].bitcast(FP8X4), lhsT_scale=w1_scales[t // 2][:, w],
                                rhs=xw[:, cols].bitcast(FP8X4), rhs_scale=xs[:, cols], start=True, stop=True)

        windows = [keep.tile([P, 2 * S], F32, name="window%d" % t) for t in range(PACK)]
        y = [w[:, 0:S] for w in windows]
        for w in windows:
            nc.gpsimd.memset(w[:, S:], 0.0)

        banks = [psum.tile([P, S], F32, name="y_bank", tag="rs%d" % e) for e in range(PACK)]
        y_half = {(t, h): banks[h][:, t * HALF : (t + 1) * HALF] for t in range(2) for h in range(2)}
        for t in range(2):
            project(y_half[t, 0], t, LEFT)
        for t in range(2):
            nc.vector.tensor_copy(y[t][:, LEFT], y_half[t, 0])
        for t in range(2):
            project(y_half[t, 1], t, RIGHT)
            nc.scalar.copy(y[t][:, RIGHT], y_half[t, 1])
        for t in range(2, PACK):
            project(banks[t][:], t, WHOLE)
            nc.scalar.copy(y[t], banks[t][:])

        y_sq = keep.tile([P, PACK, S], F32, name="y_sq")
        y_gained = keep.tile([P, PACK, S], F32, name="y_gained")
        r_all = keep.tile([P, PACK, S], F32, name="r_all")
        d_sq = keep.tile([P, PACK, S], F32, name="d_sq")
        r_sq = keep.tile([P, PACK, S], F32, name="r_sq")
        roots_turned = [keep.tile([P, PACK * P], F32, name="roots_turned%d" % b) for b in range(BLOCKS)]
        w2_bf = keep.tile([P, N * PACK], BF16, name="w2_bf", align_bytes=64)
        w2_codes = keep.tile([P, N], U32, name="w2_codes", align_bytes=64)
        w2_scales = keep.tile([P, N], U8, name="w2_scales", align_bytes=64)

        even = keep.tile([P, 2, S], F32, name="even")
        odd = keep.tile([P, 1 + BLOCKS, S], F32, name="odd")
        u_own = keep.tile([P, LAST, S], F32, name="u_own")
        d_own = keep.tile([P, LAST, S], F32, name="d_own")
        a = [(even, odd)[t % 2][:, 1, :] for t in range(PACK)]
        b = [(even, odd)[t % 2][:, 0, :] for t in range(PACK)]
        u = [u_own[:, t, :] for t in range(LAST)] + [even[:, 0, :]]
        d = [d_own[:, t, :] for t in range(LAST)] + [even[:, 1, :]]
        r = [r_all[:, t, :] for t in range(PACK)]
        numerators = odd[:, 1:, :].rearrange("p n (c t i) -> p n c t i", t=PACK, i=RUN)
        sums, roots, z_bf = {}, {}, {}

        def fetch(t, cols):
            nc.vector.tensor_copy(a[t][:, cols], windows[t][:].indirect(p1_t[:, entries(cols)]))
            nc.vector.tensor_copy(b[t][:, cols], windows[t][:].indirect(p2_t[:, entries(cols)]))
            if t < LAST:
                nc.gpsimd.tensor_tensor(u[t][:, cols], a[t][:, cols], b[t][:, cols], ALU.add)
                nc.gpsimd.tensor_tensor(d[t][:, cols], a[t][:, cols], b[t][:, cols], ALU.subtract)

        def form_r(t, cols, y_part):
            nc.vector.scalar_tensor_tensor(r[t][:, cols], y_part, LAM, u[t][:, cols], ALU.mult, ALU.add)

        def form_r_beside_gpsimd(t):
            if t < 2:
                form_r(t, LEFT, y_half[t, 0])
                form_r(t, RIGHT, y_half[t, 1])
            else:
                form_r(t, WHOLE, banks[t][:])

        def add_turned(squares, t, n, start, stop):
            nc.tensor.matmul(sums[n][:, t * P : (t + 1) * P], lhsT=squares[:, t, block(n)], rhs=ident[:],
                             is_transpose=True, start=start, stop=stop)

        def add_squares(t, cols):
            for form, squares, scale in ((d, d_sq, scale_d), (r, r_sq, SCALE_R)):
                nc.scalar.activation(squares[:, t, cols], form[t][:, cols], ACT.Square, scale=scale)
                for n in range(cols.start // BLOCK, cols.stop // BLOCK):
                    add_turned(squares, t, n, False, form is r and t == LAST)

        def round_w2(cols):
            nc.scalar.copy(w2_bf[:, cols.start * PACK : cols.stop * PACK].rearrange("p (c i j) -> p c j i", i=RUN, j=PACK),
                           w2_raw[:, :, cols].rearrange("p j (c i) -> p c j i", i=RUN))

        def inverse_root(n):
            nc.scalar.activation(roots_turned[n][:], sums[n][:], ACT.Abs_reciprocal_sqrt, bias=EPS)
            roots[n] = psum.tile([P, PACK, BLOCK], F32, name="roots", tag="rs%d" % n)
            for t in range(PACK):
                nc.tensor.transpose(roots[n][:, t, :], roots_turned[n][:, t * P : (t + 1) * P], ident[:])

        def numerator(t):
            nc.vector.scalar_tensor_tensor(numerators[:, :, :, t, :].rearrange("p n c i -> p (n c) i"),
                                           u[t].rearrange("p (c i) -> p c i", i=RUN), gain_u[:, t : t + 1],
                                           y_gained[:, t, :].rearrange("p (c i) -> p c i", i=RUN), ALU.mult, ALU.add)

        def form_z(n):
            z_bf[n] = keep.tile([P, BLOCK * PACK], BF16, name="z_bf%d" % n, align_bytes=64)
            nc.vector.tensor_tensor(z_bf[n][:].rearrange("p (c i t) -> p c t i", i=RUN, t=PACK),
                                    roots[n][:].rearrange("p t (c i) -> p c t i", i=RUN), numerators[:, n], ALU.mult)

        def second_product(n, parts):
            z_codes = keep.tile([P, BLOCK], U32, name="z_codes%d" % n, align_bytes=64)
            z_scales = keep.tile([P, BLOCK], U8, name="z_scales%d" % n, align_bytes=64)
            nc.vector.quantize_mx(out=z_codes[:].bitcast(FP8X4), scales=z_scales[:], in_=z_bf[n][:])
            tiles = N // P // len(parts)
            for part, (bank, copy_out, queue) in enumerate(parts):
                result = psum.tile([P, tiles, BLOCK], F32, name="result", tag=bank)
                for m in range(tiles):
                    w = slice((part * tiles + m) * P, (part * tiles + m + 1) * P)
                    nc.tensor.matmul_mx(out=result[:, m, :], lhsT=w2_codes[:, w].bitcast(FP8X4), lhsT_scale=w2_scales[:, w],
                                        rhs=z_codes[:].bitcast(FP8X4), rhs_scale=z_scales[:], start=True, stop=True)
                staged = keep.tile([P, tiles, BLOCK], F32, name="staged%d_%d" % (n, part))
                copy_out(staged[:], result[:])
                rows = slice(part * tiles * P, (part + 1) * tiles * P)
                queue.dma_start(out[rows, block(n)].rearrange("(m p) j -> p m j", p=P), staged[:])

        for t in range(PACK):
            nc.scalar.activation(y_sq[:, t, :], y[t], ACT.Square, scale=SCALE_Y)
        for n in range(BLOCKS):
            sums[n] = psum.tile([P, PACK * P], F32, name="sums", tag="sum%d" % n)
            for t in range(PACK):
                add_turned(y_sq, t, n, t == 0, False)
        for t in range(PACK):
            nc.scalar.activation(y_gained[:, t, :], y[t], ACT.Copy, scale=gain_y[:, t : t + 1])

        fetch(0, LEFT)
        fetch(0, RIGHT)
        fetch(1, WHOLE)
        form_r_beside_gpsimd(0)
        fetch(2, WHOLE)
        form_r_beside_gpsimd(1)
        add_squares(0, WHOLE)
        round_w2(slice(0, P))
        add_squares(1, WHOLE)
        round_w2(slice(P, N - W2_TAIL))
        fetch(LAST, WHOLE)
        form_r_beside_gpsimd(2)
        add_squares(2, WHOLE)

        for cols in (LEFT, RIGHT):
            nc.vector.tensor_tensor(u[LAST][:, cols], a[LAST][:, cols], b[LAST][:, cols], ALU.add)
        for cols in (LEFT, RIGHT):
            nc.vector.scalar_tensor_tensor(d[LAST][:, cols], a[LAST][:, cols], -2.0, u[LAST][:, cols], ALU.mult, ALU.add)
            form_r(LAST, cols, y[LAST][:, cols])
            add_squares(LAST, cols)
        round_w2(slice(N - W2_TAIL, N))
        for n in range(BLOCKS):
            inverse_root(n)
        for t in range(PACK):
            numerator(t)

        form_z(0)
        nc.vector.quantize_mx(out=w2_codes[:].bitcast(FP8X4), scales=w2_scales[:], in_=w2_bf[:])
        second_product(0, (("sum0", nc.scalar.copy, nc.sync), ("sum1", nc.scalar.copy, nc.sync)))
        form_z(1)
        form_z(2)
        second_product(1, (("sum2", nc.scalar.copy, nc.sync),))
        second_product(2, (("sum3", nc.scalar.copy, nc.sync),))
        form_z(3)
        second_product(3, (("sum0", nc.scalar.copy, nc.scalar), ("sum1", nc.vector.tensor_copy, nc.sync)))
